import numpy as np, ml_dtypes
CORES = [1,5,17,21,33,37,49,53]
N = 8
BF = ml_dtypes.bfloat16
W, V, L, F, B, TH, S, RO, SV = 3072, 1536, 256, 2, 4, 8, 4, 3, 6
def parts(rng):
    x = np.clip(rng.integers(0, 256, (N, 8, 1, W)) + rng.integers(-70, 71, (N, 8, 16, W)), 0, 255)
    q = np.clip(rng.integers(0, 200, (N, 8, 1, L)) + rng.integers(-70, 71, (N, 8, 16, L)), 0, 255)
    return x, q, rng.integers(0, W, (N, 8, W)), rng.integers(0, W, (N, 8, W)), rng.integers(0, V, (N, 8, W)), rng.integers(0, W, (N, 8, 16, V))
def pack(x, q, nx, pv, rc, u):
    return {"xd": np.ascontiguousarray(x.reshape(N, 128, W)).astype(np.float32).astype(BF), "nx": nx.astype(np.int32), "pv": pv.astype(np.int32), "rc": rc.astype(np.int32),
            "ul": np.ascontiguousarray(u.reshape(N, 128, V)).astype(np.int32), "mv": np.ascontiguousarray(q.reshape(N, 128, L)).astype(np.float32).astype(BF)}
def some(rng, n):
    return 255 * (np.argsort(rng.random((N, 8, 16, L)), axis=2) < n[:, :, None, :])
def setup_inputs(rng):
    return pack(*parts(rng))
def setup_inputs_corners(rng):
    x, q, nx, pv, rc, u = parts(rng); c = np.arange(W); sh = int(rng.integers(0, 8))
    x[..., ::64] = 255; x[..., 63::64] = 0; q[..., :8] = 0; q[..., L - 8:] = 255
    for r in range(N):
        for g in range(8):
            k = (g + 3 * r + sh) % 8
            if k == 0: nx[r, g] = c; pv[r, g] = c; rc[r, g] = c % V
            elif k == 1: nx[r, g] = np.minimum(c + 1, W - 1); pv[r, g] = np.maximum(c - 1, 0); rc[r, g] = V - 1 - c % V
            elif k == 2: nx[r, g] = (c + 1) % W; pv[r, g] = (c + W - 1) % W
            elif k == 3: nx[r, g] = 0; pv[r, g] = W - 1; rc[r, g] = V - 1
            elif k == 4: nx[r, g] = W - 1; pv[r, g] = 0; rc[r, g] = 0
            elif k == 5: u[r, g] = u[r, g, :1] + np.zeros((16, 1), np.int64)
            elif k == 6: u[r, g] = rng.choice(np.array([0, W - 1, W // 2]), (16, V))
            else: nx[r, g] = c ^ 1; pv[r, g] = c ^ 1
            if (g + r) % 2 == 0:
                z, p, e, t1, t2, t3 = [int(b) for b in 1 + rng.permutation(W - 2)[:6]]; xb, ub, i = x[r, g], u[r, g], int(rng.integers(0, 16))
                xb[:, [z, p]] = 0; xb[i, p] = 1; xb[:, [e, t1, t2, t3]] = 255; xb[i, e] = 254
                nx[r, g, [z, p, t1, t2, t3]] = z; pv[r, g, [z, t1, t3]] = t1; pv[r, g, [p, e, t2]] = t2
                ub[:, (L - 1) * SV] = p; ub[15, (L - 1) * SV] = z
                ub[:, (L - 2) * SV] = t3
                ub[:, SV] = t1; ub[15, SV] = e
    return pack(x, q, nx, pv, rc, u)
def setup_inputs_counts(rng):
    x, q, nx, pv, rc, u = parts(rng); x = np.clip(x, 1, 254)
    much = rng.permutation(np.array((256, 511, 1024, 8 * L - 1, 255, 257, 8 * L, 0)[:N]))
    hit = (np.argsort(rng.random((N, 8 * L)), axis=1) < much[:, None]).reshape(N, 8, L)
    n = np.where(hit, rng.integers(TH, 17, (N, 8, L)), rng.integers(0, TH, (N, 8, L)))
    return pack(x, some(rng, n), nx, pv, rc, u)
def setup_inputs_ends(rng):
    x = 255 * rng.integers(0, 2, (N, 8, 16, W)); m = rng.random((N, 8, 1, W)); x = np.where(m < 0.3, 0, np.where(m < 0.6, 255, x))
    fl = rng.integers(0, 2, (N, 8)); fl[0] = 0; fl[N - 1] = 0; f2 = rng.integers(0, 2, (N, 8))
    x[:, :, :, 0] = 255 * fl[:, :, None]; x[:, :, :, W - 1] = 255 * (1 - fl)[:, :, None]
    odd = (np.arange(8) % 2 == 1)[None, :, None]
    def far(hi, n):
        a = hi * rng.integers(0, 2, (N, 8, n))
        return np.where((rng.random((N, 8, n)) < 0.35) & odd, rng.integers(0, hi + 1, (N, 8, n)), a)
    nx = far(W - 1, W); pv = far(W - 1, W); rc = far(V - 1, W); u = far(W - 1, 16 * V).reshape(N, 8, 16, V)
    u[N - 1] = (W - 1) * rng.integers(0, 2, (8, 16, V)); nx[N - 1, :, 0] = 0; nx[N - 1, :, W - 1] = 0
    rc[:, :, 0] = (V - 1) * f2; rc[:, :, W - 1] = (V - 1) * (1 - f2)
    n = rng.choice(np.array([0, TH - 1, TH, 16]), (N, 8, L))
    n[0] = rng.choice(np.array([0, TH - 1, TH // 2]), (8, L)); n[N - 1] = rng.choice(np.array([16, TH]), (8, L))
    z = (L - 1) * SV; n[0, 7, L - 2:] = 0; n[N - 1, 7, L - 1] = 16
    u[0, 7, :, z] = W - 1; u[0, 7, :, z - SV] = W - 1; u[0, 7, 15, z - SV] = 0
    u[N - 1, 7, :, z] = W - 1; u[N - 1, 7, 15, z] = 0
    n[1, 7, L - 1] = 16; x[1, 7, :, 0] = 0; x[1, 7, :, 1] = 255; x[1, 7, :, 2] = 0; x[1, 7, :, W - 1] = 255
    nx[1, 7, 0] = W - 1; nx[1, 7, W - 1] = W - 1; nx[1, 7, 1] = 2; u[1, 7, :15, z] = 1; u[1, 7, 15, z] = 0
    return pack(x, some(rng, n), nx, pv, rc, u)
def setup_inputs_near(rng):
    x, q, nx, pv, rc, u = parts(rng); b = rng.integers(0, 255, (N, 8, 1, 1)); b[0, 0] = 0; b[1, 1] = 254
    x = b + (rng.random((N, 8, 16, W)) < rng.choice(np.array([0.2, 0.5, 0.8]), (N, 8, 1, W)))
    q = b + (rng.random((N, 8, 16, L)) < rng.choice(np.array([0.2, 0.5, 0.8, 1.0]), (N, 8, 1, L)))
    few = rng.integers(0, W, (N, 8, 64)); u = np.take_along_axis(few, rng.integers(0, 64, (N, 8, 16 * V)), 2).reshape(N, 8, 16, V)
    return pack(x, q, nx, pv, rc, u)
def setup_inputs_spread(rng):
    x = (np.exp2(8 * rng.random((N, 8, 1, W))) * rng.random((N, 8, 16, W))).astype(np.int64)
    q = (np.exp2(8 * rng.random((N, 8, 1, L))) * rng.random((N, 8, 16, L))).astype(np.int64)
    def skew(hi, n):
        return np.minimum((hi * rng.random((N, 8, n)) ** rng.choice(np.array([1, 2, 4]), (N, 8, 1))).astype(np.int64), hi - 1)
    return pack(np.minimum(x, 255), np.minimum(q, 255), skew(W, W), skew(W, W), skew(V, W), skew(W, 16 * V).reshape(N, 8, 16, V))
def check_inputs(d):
    bad = []
    for k, lo, hi in (("xd", 0, 255), ("nx", 0, W - 1), ("pv", 0, W - 1), ("rc", 0, V - 1), ("ul", 0, W - 1), ("mv", 0, 255)):
        a = np.asarray(d[k]).astype(np.float64)
        if not (np.min(a) >= lo and np.max(a) <= hi): bad.append("range of " + k)
        elif np.any(a != np.floor(a)): bad.append("whole numbers in " + k)
    return bad
def lowest(n):
    same = n[:, :, :, None] == n[:, :, None, :]
    return ~np.any(same & np.tril(np.ones((L, L), bool), -1), axis=3)
def reference(xd, nx, pv, rc, ul, mv):
    X = np.ascontiguousarray(xd.astype(np.float32).astype(np.int32).reshape(N, 8, 16, W).transpose(0, 1, 3, 2))
    q = np.ascontiguousarray(mv.astype(np.float32).astype(np.int32).reshape(N, 8, 16, L).transpose(0, 1, 3, 2))
    nxt, pre, rec = nx.astype(np.int64), pv.astype(np.int64), rc.astype(np.int64)
    U = ul.astype(np.int64).reshape(N, 8, 16, V); v = np.zeros((N, 8, L), np.int64) + SV * np.arange(L)
    R3, G3 = np.arange(N)[:, None, None], np.arange(8)[None, :, None]; R4, G4 = R3[..., None], G3[..., None]
    for t in range(RO):
        d = np.take_along_axis(U, v[:, :, None, :], 3)
        score = np.add.reduce(np.abs(X[R4, G4, d] - q[:, :, None]), axis=4)
        cleared = np.zeros(d.shape, bool); c = d
        for f in range(F):
            c = nxt[R4, G4, c]
            cleared = cleared | (np.add.reduce((X[R4, G4, c] < q[:, :, None]).astype(np.int32), axis=4) >= TH)
        none = np.all(cleared, axis=2)
        k = np.where(none, np.argmax(score, axis=2), np.argmin(np.where(cleared, 2 ** 20, score), axis=2))
        a = np.take_along_axis(d, k[:, :, None, :], 2)[:, :, 0]; go = np.ones(a.shape, bool)
        for s in range(B):
            b = pre[R3, G3, a]
            go = go & (np.add.reduce((X[R3, G3, b] < q).astype(np.int32), axis=3) < TH)
            a = np.where(go, b, a)
        w = rec[R3, G3, a]
        A = np.add.reduce(none.reshape(N, -1).astype(np.int32), axis=1) & 255
        z = (q + A[:, None, None, None]) >> 1
        xn = (X[R3, G3, a] + q + 1) >> 1; nn = nxt[R3, G3, nxt[R3, G3, a]]
        r, g, i = np.nonzero(lowest(v)); U[r, g, k[r, g, i], v[r, g, i]] = a[r, g, i]
        r, g, i = np.nonzero(lowest(a)); X[r, g, a[r, g, i]] = xn[r, g, i]; nxt[r, g, a[r, g, i]] = nn[r, g, i]
        v = w + 0; q = z + 0
        for h in range(1, S):
            s = 1 + (t + h - 1) % (N - 1)
            v[:, :, h::S] = np.roll(w, s, axis=0)[:, :, h::S]; q[:, :, h::S] = np.roll(z, s, axis=0)[:, :, h::S]
    return {"yu": U.reshape(N, 128, V).astype(np.float32), "yx": np.ascontiguousarray(X.transpose(0, 1, 3, 2)).reshape(N, 128, W).astype(np.float32).astype(BF),
            "yv": v.astype(np.float32), "yq": np.ascontiguousarray(q.transpose(0, 1, 3, 2)).reshape(N, 128, L).astype(np.float32).astype(BF)}

from concourse.mybir import AluOpType, AxisListType, ActivationFunctionType

OP, AF = AluOpType, ActivationFunctionType
NR = 3
BIG = 131072.0
SHARE = ((3, 0), (3, 1))
SBANK = ("P4", "P5", "P3", "P6")

SCRATCH = {}


def _buf(dtype, **names):
    for k, n in names.items():
        SCRATCH[k] = ("sbuf", [128, n], dtype)


_buf("bfloat16", X=3328, X1=3072, X2=3072, TT=15360, ZZ=3072, NXR=3328, BHB=768, BLB=768, Q16=4096, QW=1024,
     DF=4096, AB=4096, L1=4096, L2=4096, LW=1024, XG=2048, EA=2176, EV=2176, EW=2176, NFB=16, E16=16)
_buf("int32", ULI=1536, B4=768, BHI=768, BLI=768, KI=16, I192=192, I16=16, IJL=16, I32=32, I64=64, IQ4=64)
_buf("uint16", NXL=192, PVL=192, C64=64, Q4L=64, DL=256, BLU=64)
_buf("float16", DI=256, OHD=256, OHA=256, AR16=256, UH=144, IDH=128, IDMH=128)
_buf("float32", ULF=1792, IN144=144, IG16=128)
for _t in range(NR + 1):
    SCRATCH["QJ%d" % _t] = ("sbuf", [128, 256], "bfloat16")
    SCRATCH["VL%d" % _t] = ("sbuf", [128, 32], "uint16")
    if _t < NR:
        SCRATCH["ZB%d" % _t] = ("sbuf", [128, 256], "bfloat16")
        SCRATCH["MW%d" % _t] = ("sbuf", [128, 32], "uint16")
for _k in range(8):
    SCRATCH["P%d" % _k] = ("psum", [128, 512], "float32")
_PACK, _WIDTH = {}, {}
for _w, _names, _dt, _n, _u in (
        ("sm", "IP P16 G16 F2 R4 RM G15 G12 C192 C96 C16 CQ WA WW WP W3 T1 T2 NRED AM NP", "float32", 8, 1),
        ("ci", "IPI PI F2I R4I RMI NI", "int32", 8, 1),
        ("lu", "QIL IJU KU AU O2 AU2 OFA OFV VPU N1U", "uint16", 16, 16),
        ("lf", "DUA DUV IDU IDV A0F AC A2F OM NV VF OMV YV", "float32", 16, 16),
        ("mat", "U U16 UC UA UW UP U3", "bfloat16", 144, 144),
        ("sq", "BB BB4 TR RA ONE CB CZ IDP IDM CM4", "bfloat16", 128, 128),
        ("ff", "K16 KB2 DB D0 MK KB W1 W2 KEY CM CS CMV CSV UV", "float32", 256, 256),
        ("bb", "QM QI1 QI2 FB GB VJ VG N1B NNB ON KPB", "bfloat16", 256, 256),
        ("ii", "RI ZI XI XS", "int32", 256, 256),
        ("fs", "IS64 DW DS N5 S1 S2", "float32", 64, 64)):
    for _j, _nm in enumerate(_names.split()):
        _PACK[_nm] = (_w, _j * _n)
        _WIDTH[_nm] = _u
    SCRATCH[_w] = ("sbuf", [128, _n * len(_names.split())], _dt)

NDMA = 40
SEMAPHORES = ["qV", "qS", "qP", "qG", "sent"] + ["d%d" % _k for _k in range(NDMA)]
for _t in range(NR):
    for _h in range(1, 4):
        SEMAPHORES += ["z%d%d" % (_t, _h), "w%d%d" % (_t, _h)]


def shift(t, h):
    return 1 + (t + h - 1) % 7


def rank_program(g, core, T, topo):
    me = T.rank_of(core)
    if me is None:
        return
    N = len(T.cores)
    ENG = {"V": g.vector, "S": g.scalar, "P": g.tensor, "G": g, "sync": g.sync, "act": g.scalar}
    cnt = {"V": 0, "S": 0, "P": 0, "G": 0}
    know = {"V": {}, "S": {}, "P": {}, "G": {}, "sync": {}}
    snap = {}
    unit = {"V": 1, "S": 1, "P": 1, "G": 1}
    total = {}
    log = {}
    nd = [0]
    sent = [0]

    def v(name, lo=0, hi=None, step=1):
        w, b = _PACK.get(name, (name, 0))
        if hi is None: hi = _WIDTH[name] if name in _PACK else T[w].shape[1]
        lo, hi = lo + b, hi + b
        ap = T[w][:, lo:hi:step] if step != 1 else T[w][:, lo:hi]
        return (ap, [(w, lo, hi, step, None)], [])

    def rows(name, f, lo, hi):
        return (T[name][f:128:16, lo:hi], [(name, lo, hi, 1, f)], [])

    def ind(win, off):
        return (win[0].indirect(off[0]), win[1], off[1])

    def order(q, w, r):
        need = {}
        def dep(tok):
            if tok[0] == q == "P": return
            if know[q].get(tok[0], 0) < tok[1]: need[tok[0]] = max(need.get(tok[0], 0), tok[1])
        for keys, wr in ((w, True), (r, False)):
            for (nm, lo, hi, stp, prt) in keys:
                ps = nm[0] == "P" and nm[1:].isdigit()
                for (l2, h2, kind, tok, s2, p2) in log.get(nm, []):
                    if ps:
                        if tok[0] != q or (kind == "w" and not wr): dep(tok)
                    elif l2 < hi and lo < h2 and (kind == "w" or wr):
                        if prt is not None and p2 is not None and prt != p2: continue
                        if stp == s2 and stp > 1 and (lo - l2) % stp: continue
                        dep(tok)
        for a in sorted(need):
            if any(b != a and snap.get((b, need[b]), {}).get(a, 0) >= need[a] for b in need): continue
            ENG[q].wait_ge(T.sem["q" + a if a in cnt else a], need[a] * unit[a])
        for a in need:
            for b, n in snap.get((a, need[a]), {}).items(): know[q][b] = max(know[q].get(b, 0), n)
            know[q][a] = max(know[q].get(a, 0), need[a])

    def note(tok, w, r):
        for keys, kind in ((w, "w"), (r, "r")):
            for (nm, lo, hi, stp, prt) in keys:
                ps = nm[0] == "P" and nm[1:].isdigit()
                if ps: lo, hi = 0, 512
                L = log.setdefault(nm, [])
                if ps and kind == "r":
                    L[:] = [e for e in L if e[2] == "w" and e[3][0] == "P"][-1:] + [(lo, hi, "r", tok, 1, None)]
                else:
                    if kind == "w" and stp == 1 and prt is None: L[:] = [e for e in L if not (lo <= e[0] and e[1] <= hi)]
                    L.append((lo, hi, kind, tok, stp, prt))

    def emit(q, fn, outs, ins):
        w, r = [], []
        for o in outs: w += o[1]; r += o[2]
        for i in ins: r += i[1] + i[2]
        order(q, w, r)
        cnt[q] += 1
        fn().then_inc(T.sem["q" + q], 1)
        now = dict(know[q]); now[q] = cnt[q]
        snap[(q, cnt[q])] = now
        note((q, cnt[q]), w, r)

    def dma(out, in_, q="sync"):
        qk = {"sync": "sync", "act": "S"}[q]
        w = out[1] if isinstance(out, tuple) else []
        r = in_[1] if isinstance(in_, tuple) else []
        order(qk, w, r)
        nm = "d%d" % nd[0]; nd[0] += 1
        o = out[0] if isinstance(out, tuple) else out
        i = in_[0] if isinstance(in_, tuple) else in_
        ENG[q].dma_start(o, i).then_inc(T.sem[nm], 16)
        unit[nm] = 16; total[nm] = 1
        snap[(nm, 1)] = dict(know[qk])
        note((nm, 1), w, r)

    def remote(kind, t, h, dst_view, src_view):
        d = T.cores[(me + shift(t, h)) % N]
        order("G", [], src_view[1])
        rid, pid, _s = topo.addr(d)
        es = topo.engines(core, d)[:8]
        nm = "%s%d%d" % (kind, t, h)
        g.remote_dma(dst_view[0], src_view[0], T.sem[nm], T.sem.sent, pid, rid, sum(1 << e for e in es))
        sent[0] += len(es)
        src = T.cores[(me - shift(t, h)) % N]
        unit[nm] = len(topo.engines(src, core)[:8]); total[nm] = 1
        snap[(nm, 1)] = {}
        note((nm, 1), dst_view[1], [])

    def cp(o, i): emit("V", lambda: g.vector.tensor_copy(o[0], i[0]), [o], [i])
    def tt(o, a, b, op): emit("V", lambda: g.vector.tensor_tensor(o[0], a[0], b[0], op), [o], [a, b])
    def ts(o, a, s1, op0, s2=None, op1=None):
        ex = [s for s in (s1, s2) if isinstance(s, tuple)]
        x1 = s1[0] if isinstance(s1, tuple) else s1
        x2 = s2[0] if isinstance(s2, tuple) else s2
        if op1 is None: emit("V", lambda: g.vector.tensor_scalar(o[0], a[0], x1, None, op0), [o], [a] + ex)
        else: emit("V", lambda: g.vector.tensor_scalar(o[0], a[0], x1, x2, op0, op1), [o], [a] + ex)
    def scan(o, d0, d1, init, op0, op1): emit("V", lambda: g.vector.tensor_tensor_scan(o[0], d0[0], d1[0], init, op0, op1), [o], [d0, d1])
    def rsum(o, i): emit("V", lambda: g.vector.tensor_reduce(o[0], i[0], AxisListType.X, OP.add), [o], [i])
    def fill(o, c): emit("V", lambda: g.vector.memset(o[0], c), [o], [])
    def act(o, i, f=AF.Identity, bias=0.0, scale=1.0):
        ex = [s for s in (bias, scale) if isinstance(s, tuple)]
        b = bias[0] if isinstance(bias, tuple) else bias
        s = scale[0] if isinstance(scale, tuple) else scale
        emit("S", lambda: g.scalar.activation(o[0], i[0], f, bias=b, scale=s), [o], [i] + ex)
    def mm(o, l, r, start, stop): emit("P", lambda: g.tensor.matmul(o[0], l[0], r[0], start, stop), [o], [l, r])
    def iota(o, pat, base=0, cm=0, small=True):
        if small: emit("G", lambda: g.iota(o[0], pat, base, cm, allow_small_or_imprecise_dtypes=True), [o], [])
        else: emit("G", lambda: g.iota(o[0], pat, base, cm), [o], [])
    def keep(o, i, pat, op, base, cm): emit("G", lambda: g.affine_select(o[0], i[0], pat, op, 0.0, base, cm), [o], [i])
    def usl(name, r): return v(name, 15 - r, 143 - r)

    def diag(bank, mat, src, n):
        for r in range(16):
            mm(v(bank, 0, n), usl(mat, r), v(src, r, 16 * n, 16), r == 0, r == 15)

    dma(v("B4", 576, 768), T.nx[:])
    dma(v("B4", 384, 576), T.pv[:], "act")
    dma(v("QM"), T.mv[:])
    dma(v("ULI"), T.ul[:])
    dma(v("X", 0, 3072), T.xd[:], "act")
    dma(v("B4", 192, 384), T.rc[:])

    fill(v("NXR", 0, 3072), 0.0)
    fill(v("ON"), 1.0)
    iota(v("IPI"), [[1, 1]], 0, 1, False)
    iota(v("IP"), [[1, 1]], 0, 1)
    iota(v("IN144"), [[1, 144]])
    iota(v("IJL"), [[1, 4], [4, 4]], 0, 0, False)
    iota(v("I64"), [[1, 64]], 0, 0, False)
    iota(v("I32"), [[6, 4], [24, 8]], 0, 0, False)
    iota(v("I192"), [[1, 192]], 0, 0, False)
    iota(v("K16"), [[0, 16], [1, 16]])
    iota(v("IG16"), [[16, 8], [0, 16]])
    iota(v("I16"), [[1, 16]], 0, 0, False)
    iota(v("IQ4"), [[16, 4], [64, 4], [4, 4]], 0, 0, False)
    iota(v("IDU"), [[16, 16]], 3072, 0)
    iota(v("IDV"), [[16, 16]], 1536, 0)
    iota(v("IS64"), [[0, 16], [1, 4]])
    keep(v("IDP"), v("ON", 0, 128), [[-1, 128]], OP.is_equal, 0, 1)
    iota(v("ZZ"), [[0, 3072]])

    def halves(lo, hi):
        ts(v("BHI", lo, hi), v("B4", lo, hi), 6, OP.arith_shift_right)
        ts(v("BLI", lo, hi), v("B4", lo, hi), 63, OP.bitwise_and)
        cp(v("BHB", lo, hi), v("BHI", lo, hi))
        cp(v("BLB", lo, hi), v("BLI", lo, hi))

    def weights(nm, k):
        ts(v("T1"), v("P16"), k, OP.is_equal, 64.0, OP.mult)
        ts(v("T2"), v("P16"), k + 1, OP.is_equal)
        tt(v(nm), v("T1"), v("T2"), OP.add)

    def spread(t, hs):
        for h in hs:
            act(v("Q16", 1024 * h, 1024 * h + 1024), ind(v("QJ%d" % t, 64 * h, 64 * h + 64), v("C64")))

    ts(v("PI"), v("IPI"), 15, OP.bitwise_and)
    cp(v("P16"), v("PI"))
    ts(v("C16"), v("P16"), 16.0, OP.mult)
    ts(v("IJU"), v("IJL"), v("C16"), OP.add)
    cp(v("C64"), v("I64"))
    halves(576, 768)
    dma(rows("NXR", 0, 0, 3072), v("BHB", 576, 768))
    dma(rows("NXR", 1, 0, 3072), v("BLB", 576, 768))
    weights("WA", 0.0)
    tt(v("G16"), v("IP"), v("P16"), OP.subtract)
    ts(v("G15"), v("G16"), 15.0, OP.add)
    ts(v("U"), v("IN144"), v("G15"), OP.is_equal)
    act(v("QJ0"), ind(v("QM"), v("IJU")))
    act(v("UA"), v("U"), scale=v("WA"))
    ts(v("C96"), v("P16"), 96.0, OP.mult)
    ts(v("VL0"), v("I32"), v("C96"), OP.add)
    fill(v("TT", 0, 3072), 0.0)
    halves(384, 576)
    dma(rows("TT", 4, 0, 3072), v("BHB", 384, 576))
    dma(rows("TT", 5, 0, 3072), v("BLB", 384, 576))
    weights("WP", 4.0)
    spread(0, range(1))
    act(v("UP"), v("U"), scale=v("WP"))
    spread(0, range(1, 3))
    diag("P3", "UA", "NXR", 192)
    diag("P7", "UP", "TT", 192)

    def consts2():
        ts(v("C192"), v("P16"), 192.0, OP.mult)
        ts(v("B4", 0, 192), v("I192"), v("C192"), OP.add)
        halves(0, 384)
        for k in range(2):
            dma(rows("TT", 2 * k, 0, 3072), v("BHB", 192 * k, 192 * k + 192))
            dma(rows("TT", 2 * k + 1, 0, 3072), v("BLB", 192 * k, 192 * k + 192))
        weights("WW", 2.0)
        ts(v("NP"), v("P16"), -1.0, OP.mult)
        ts(v("IDM"), v("IDP"), -1.0, OP.mult)
        act(v("U16"), v("U"), scale=16.0)
        act(v("UC"), v("U"), scale=1048576.0)
        act(v("KPB"), v("K16"))
        fill(v("CB"), -61440.0)
        cp(v("PVL"), v("P7", 0, 192))

    def late_consts():
        act(v("UW"), v("U"), scale=v("WW"))
        act(v("D0"), v("K16"), AF.Sign)
        act(v("DB"), v("D0"), scale=-524288.0, bias=524288.0)
        act(v("KB2"), v("K16"), scale=2.0, bias=BIG)
        act(v("MK"), v("K16"), AF.Square, bias=v("NP"))
        act(v("MK"), v("MK"), AF.Relu, scale=-1.0, bias=1.0)
        act(v("DS"), v("IS64"), AF.Sign)
        act(v("DW"), v("DS"), scale=-3072.0, bias=3072.0)
        act(v("DUA"), v("IDU"), bias=v("P16"))
        act(v("DUV"), v("IDV"), bias=v("P16"))
        ts(v("R4I"), v("PI"), 2, OP.arith_shift_right)
        ts(v("F2I"), v("PI"), 1, OP.arith_shift_right)
        ts(v("RMI"), v("PI"), 3, OP.bitwise_and)
        cp(v("R4"), v("R4I"))
        cp(v("F2"), v("F2I"))
        cp(v("RM"), v("RMI"))
        cp(v("UH"), v("U"))
        cp(v("IDH"), v("IDP"))
        ts(v("IDMH"), v("IDP"), -1.0, OP.mult)
        ts(v("T1"), v("F2"), -2.0, OP.mult, v("P16"), OP.add)
        ts(v("T1"), v("T1"), -63.0, OP.mult, 64.0, OP.add)
        ts(v("W3"), v("P16"), 8.0, OP.is_lt, v("T1"), OP.mult)
        tt(v("G12"), v("G16"), v("F2"), OP.add)
        ts(v("G12"), v("G12"), 12.0, OP.add)
        ts(v("U3"), v("IN144"), v("G12"), OP.is_equal, v("W3"), OP.mult)
        ts(v("BB"), v("IG16"), v("G16"), OP.is_equal)
        act(v("BB4"), v("BB"), scale=4096.0)
        act(v("RA"), v("BB"), scale=v("WA"))
        keep(v("TR"), v("BB4"), [[1, 128]], OP.is_gt, 0, -1)
        fill(v("ONE"), 1.0)
        fill(v("CZ"), 0.0)
        fill(v("CM4"), -1.0 / 4096)
        ts(v("E16"), v("IN144", 0, 16), v("P16"), OP.is_equal)
        ts(v("Q4L"), v("IQ4"), v("R4"), OP.add)
        ts(v("CQ"), v("RM"), 64.0, OP.mult)
        ts(v("T1"), v("R4"), 16.0, OP.mult)
        tt(v("CQ"), v("CQ"), v("T1"), OP.add)
        ts(v("QIL"), v("I16"), v("CQ"), OP.add)

    def table(q, m):
        o, w = v("TT", 3072 * m, 3072 * m + 3072), v("TT", 3072 * m - 3072, 3072 * m)
        if q == "V": cp(o, ind(w, v("PVL")))
        else: act(o, ind(w, v("PVL")))
        for f in range(2):
            dma(rows("ZZ", 2 * m - 2 + f, 0, 3072), rows("TT", f, 3072 * m, 3072 * m + 3072))

    def lane_q(t):
        act(v("QW"), ind(v("QJ%d" % t), v("Q4L")))
        act(v("QI%d" % (1 + t % 2)), ind(v("QJ%d" % t), v("QIL")), bias=1.0)

    def eo(p): return 256 * p - 8 * p * (p - 1)

    def dedupe_mm(bank, e, ps):
        for p in ps:
            if p == 0: mm(v(bank, 0, 256), v("CZ"), v("ON"), True, False)
            if p < 15: mm(v(bank, 16 * p + 16, 256), v("BB4"), v(e, eo(p) + 16, eo(p + 1)), False, False)
            mm(v(bank, 16 * p, 16 * p + 16), v("TR"), v(e, eo(p), eo(p) + 16), False, p == 15)

    def dedupe_off(bank, cm, cs, om, dump, num, off):
        tt(v(cm), v(bank, 0, 256), v("MK"), OP.mult)
        scan(v(cs), v("D0"), v(cm), 0.0, OP.mult, OP.add)
        tt(v(om), v(cs, 15, 256, 16), v(dump), OP.min)
        tt(v(off), v(om), v(num), OP.max)

    def test(x, out, h, op, n=1024):
        tt(v(out, 1024 * h, 1024 * h + n), ind(v(x, 0, 3072), v("DL", 64 * h, 64 * h + n // 16)), v("Q16", 1024 * h, 1024 * h + n), op)

    def sums(bank, mat, src, h, last):
        for c in range(4):
            mm(v(bank, 0, 256), usl(mat, 4 * c + h), v(src, 1024 * h + 256 * c, 1024 * h + 256 * c + 256), False, last and c == 3)

    for t in range(NR):
        Q, Qn, VLt, Vn = "QJ%d" % t, "QJ%d" % (t + 1), "VL%d" % t, "VL%d" % (t + 1)
        first, lastr = t == 0, t == NR - 1
        UT = v("ULI") if first else v("ULF", 0, 1536)

        def places(h): cp(v("DL", 64 * h, 64 * h + 64), ind(UT, v(VLt, 8 * h, 8 * h + 4)))
        places(0)
        test("X", "DF", 0, OP.subtract)
        if first: cp(v("NXL"), v("P3", 0, 192))
        act(v("X1"), ind(v("X", 0, 3072), v("NXL")))
        if first: spread(0, range(3, 4))
        act(v("X2"), ind(v("X1"), v("NXL")))
        for h in range(1, 4):
            places(h)
            n = 1024 - 512 * len([1 for x in SHARE if x[0] == h])
            if n: test("X", "DF", h, OP.subtract, n)
        if first:
            consts2()
            late_consts()
            table("V", 1)
            table("V", 2)
        for h in range(4):
            act(v("VJ", 64 * h, 64 * h + 64), ind(v("TT", 0, 3072), v(VLt, 8 * h, 8 * h + 4)))
        for r in [4 * c + k for k in range(4) for c in range(4)]:
            b = 64 * (r % 4) + 16 * (r // 4)
            mm(v("P7", 0, 16), usl("UA", r), v("VJ", b, b + 16), r == 0, r == 15)
        for j, (h, k) in enumerate(SHARE):
            act(v("XG", 512 * j, 512 * j + 512), ind(v("X", 0, 3072), v("DL", 64 * h + 32 * k, 64 * h + 32 * k + 32)))
        for h in range(4):
            n = 1024 - 512 * len([1 for x in SHARE if x[0] == h])
            if n: act(v("AB", 1024 * h, 1024 * h + n), v("DF", 1024 * h, 1024 * h + n), AF.Abs)
        mm(v("P1", 0, 256), v("CB"), v("ON"), True, False)
        mm(v("P2", 0, 256), v("CB"), v("ON"), True, False)
        mm(v("P0", 0, 256), v("IDP"), v("KPB"), True, False)
        for h in range(4):
            test("X1", "L1", h, OP.is_lt)
            sums("P1", "UC", "L1", h, h == 3)
            if h == 1:
                for j, (hs, k) in enumerate(SHARE):
                    mm(v(SBANK[j]), v("IDP"), v("XG", 512 * j, 512 * j + 512), True, False)
                    mm(v(SBANK[j]), v("IDM"), v("Q16", 1024 * hs + 512 * k, 1024 * hs + 512 * k + 512), False, True)
                for j, (hs, k) in enumerate(SHARE):
                    act(v("AB", 1024 * hs + 512 * k, 1024 * hs + 512 * k + 512), v(SBANK[j]), AF.Abs)
        cp(v("VPU"), v("P7", 0, 16))
        act(v("VF"), v("P7", 0, 16))
        act(v("NV"), v("P7", 0, 16), scale=-1.0)
        act(v("VG"), ind(v("TT", 0, 3072), v("VPU")))
        for h in range(4):
            sums("P0", "U16", "AB", h, h == 3)
        mm(v("P6", 0, 256), v("RA"), v("VG"), True, True)
        if first:
            lane_q(0)
            table("S", 3)
            table("S", 4)
        for h in range(2):
            test("X2", "L2", h, OP.is_lt)
            sums("P2", "UC", "L2", h, False)
        test("X2", "L2", 2, OP.is_lt)
        sums("P2", "UC", "L2", 2, False)
        for p in range(16):
            act(v("EV", eo(p), eo(p + 1)), v("P6", 16 * p, 256), AF.Square, bias=v("NV", p, p + 1))
        act(v("EW"), v("EV"), AF.Relu, scale=-1.0, bias=1.0)
        test("X2", "L2", 3, OP.is_lt)
        sums("P2", "UC", "L2", 3, True)
        ts(v("DI"), ind(UT, v("VPU")), -1536.0, OP.add)
        tt(v("KB"), v("KB2"), v("P0", 0, 256), OP.subtract)
        tt(v("W1"), v("P1", 0, 256), v("KB"), OP.min)
        tt(v("P4", 0, 256), v("W1"), v("P0", 0, 256), OP.max)
        tt(v("W2"), v("P2", 0, 256), v("KB"), OP.min)
        tt(v("KEY"), v("W2"), v("P4", 0, 256), OP.max)
        scan(v("RI"), v("DB"), v("KEY"), 1000000.0, OP.add, OP.min)
        ts(v("KI"), v("RI", 15, 256, 16), 15, OP.bitwise_and)
        cp(v("KU"), v("KI"))
        tt(v("OHD"), ind(v("E16"), v("KU")), v("DI"), OP.mult)
        diag("P3", "UH", "OHD", 16)
        ts(v("NFB"), v("RI", 15, 256, 16), 65536.0, OP.is_ge)
        mm(v("P1", 0, 16), v("ONE"), v("NFB"), True, False)
        mm(v("P1", 0, 16), v("CM4"), v("ON", 0, 16), False, True)
        if first: cp(v("ULF", 0, 1536), v("ULI"))
        ts(v("AU"), v("P3", 0, 16), 1536.0, OP.add)
        cp(v("FB"), ind(v("ZZ"), v("AU")))
        for ch in range(4):
            for r4 in range(4):
                b = 64 * ch + 16 * r4
                mm(v("P4", ch, 64, 4), v("U3", 12 - 4 * r4, 140 - 4 * r4), v("FB", b, b + 16), r4 == 0, r4 == 3)
        rsum(v("NRED"), v("P1", 0, 16))
        ts(v("NI"), v("NRED"), 1.0 / 256, OP.mult, -127.0 / 256, OP.add)
        ts(v("AM"), v("NI"), -256.0, OP.mult, v("NRED"), OP.add)
        ts(v("A0F"), v("P3", 0, 16), 1536.0, OP.add)
        ts(v("ZI"), v(Q), v("AM"), OP.add, 0.5, OP.mult)
        cp(v("BLU"), v("P4", 0, 64))
        for k in range(2):
            tt(v("LW", 512 * k, 512 * k + 512), ind(v("X", 0, 3072), v("BLU", 32 * k, 32 * k + 32)), v("QW", 512 * k, 512 * k + 512), OP.is_lt)
            for r in range(8 * k, 8 * k + 8):
                mm(v("P5", 0, 64), usl("U", r), v("LW", 64 * r, 64 * r + 64), r == 0, r == 15)
        cp(v("ZB%d" % t), v("ZI"))
        for h in range(1, 4):
            remote("z", t, h, v(Qn, 64 * h, 64 * h + 64), v("ZB%d" % t, 64 * h, 64 * h + 64))
        act(v(Qn, 0, 64), v("ZB%d" % t, 0, 64))
        if not lastr: spread(t + 1, range(1))
        ts(v("N5"), v("P5", 0, 64), 7.5, OP.is_lt, 3072.0, OP.mult)
        scan(v("S1"), v("DW"), v("N5"), 0.0, OP.max, OP.min)
        scan(v("S2"), v("DS"), v("S1"), 0.0, OP.mult, OP.add)
        tt(v("O2"), v("S2", 3, 64, 4), v("A0F"), OP.add)
        cp(v("GB"), ind(v("TT"), v("O2")))
        for p in range(16):
            mm(v("P6", 0, 16), usl("UW", p), v("GB", 16 * p, 16 * p + 16), p == 0, p == 15)
        diag("P7", "UA", "GB", 16)
        mm(v("P4", 0, 256), v("RA"), v("GB"), True, True)
        for h in range(1, 4):
            cp(v("MW%d" % t, 8 * h, 8 * h + 4), v("P6", h, 16, 4))
            remote("w", t, h, v(Vn, 8 * h, 8 * h + 4), v("MW%d" % t, 8 * h, 8 * h + 4))
        cp(v(Vn, 0, 4), v("P6", 0, 16, 4))
        cp(v("AU2"), v("P7", 0, 16))
        ts(v("AC"), v("P7", 0, 16), -1536.0, OP.add)
        act(v("A2F"), v("P7", 0, 16))
        ts(v("AR16"), v("P4", 0, 256), -1536.0, OP.add)
        if not lastr:
            act(v("N1B"), ind(v("NXR", 0, 3072), v("AU2")))
            diag("P6", "UA", "N1B", 16)
        for p in range(16):
            ts(v("EA", eo(p), eo(p + 1)), v("AR16", 16 * p, 256), v("AC", p, p + 1), OP.is_equal)
            dedupe_mm("P5", "EA", range(p, p + 1))
            if p == 9 and not lastr:
                cp(v("N1U"), v("P6", 0, 16))
                act(v("NNB"), ind(v("NXR", 0, 3072), v("N1U")))
                spread(t + 1, range(1, 4))
        dedupe_mm("P0", "EW", range(16))
        tt(v("XI"), ind(v("X", 0, 3072), v("AU2")), v("QI%d" % (1 + t % 2)), OP.add)
        ts(v("XS"), v("XI"), 1, OP.arith_shift_right)
        tt(v("OHA"), ind(v("E16"), v("KU")), v("AR16"), OP.mult)
        mm(v("P7", 0, 256), v("IDH"), v("DI"), True, False)
        mm(v("P7", 0, 256), v("IDMH"), v("OHD"), False, False)
        mm(v("P7", 0, 256), v("IDH"), v("OHA"), False, True)
        act(v("UV"), v("P7", 0, 256), bias=1536.0)
        if not lastr: lane_q(t + 1)
        dedupe_off("P5", "CM", "CS", "OM", "DUA", "A2F", "OFA")
        if not lastr:
            cp(ind(v("NXR"), v("OFA")), v("NNB"))
            diag("P3", "UA", "NXR", 192)
        cp(ind(v("X"), v("OFA")), v("XS"))
        if lastr: dma(T.yx[:], v("X", 0, 3072), "act")
        dedupe_off("P0", "CMV", "CSV", "OMV", "DUV", "VF", "OFV")
        cp(ind(v("ULF"), v("OFV")), v("UV"))
        if not lastr: cp(v("NXL"), v("P3", 0, 192))
        if lastr: dma(T.yu[:], v("ULF", 0, 1536))
    VE, QE = "VL%d" % NR, "QJ%d" % NR
    act(v("QI1"), ind(v(QE), v("QIL")))
    dma(T.yq[:], v("QI1"), "act")
    for h in range(4):
        cp(v("YV", h, 16, 4), v(VE, 8 * h, 8 * h + 4))
    dma(T.yv[:], v("YV"))
    for q in ("V", "S", "P", "G"):
        g.wait_ge(T.sem["q" + q], cnt[q])
    for nm in sorted(total):
        g.wait_ge(T.sem[nm], unit[nm])
    g.wait_ge(T.sem.sent, sent[0])
